import numpy as np
import ml_dtypes


def mxq(x, axis, fmt="e4m3"):
    dtype, down = {"e4m3": (ml_dtypes.float8_e4m3fn, 7), "e5m2": (ml_dtypes.float8_e5m2, 14)}[fmt]
    v = np.moveaxis(np.asarray(x, np.float32).astype(ml_dtypes.bfloat16).astype(np.float64), axis, -1)
    blocks = v.reshape(v.shape[:-1] + (-1, 32))
    amax = np.abs(blocks).max(-1, keepdims=True)
    byte = np.maximum(np.where(amax > 0, np.frexp(amax)[1] - 1 + 127, 0) - down, 1)
    scale = np.exp2(byte - 127.0)
    codes = (blocks / scale).astype(np.float32).astype(dtype).astype(np.float64)
    return np.moveaxis((codes * scale).reshape(v.shape), -1, axis)


WIDE = False


def mx_kscale(k):
    if not WIDE:
        return np.ones(k)
    levels = np.array([10, -10, 5, -5, 0])
    if k % 512:
        return np.exp2(np.random.permutation(np.resize(levels, k // 32))).repeat(32)
    a = np.empty((k // 512, 16))
    for p in range(k // 512):
        a[p, :8] = np.random.permutation(np.resize(levels, 8))
        for g in range(8):
            far = levels[np.abs(levels - a[p, g]) >= 10]
            a[p, g + 8] = far[np.random.randint(len(far))]
    return np.exp2(a.ravel()).repeat(32)


def f64(x):
    return np.asarray(x).astype(np.float64)


def striped(idx):
    return np.tile(idx.reshape(-1, 16).T, (8, 1)).astype(np.uint16)


def unstriped(offs):
    return offs[:16].T.reshape(-1).astype(np.int64)


def pack_weight(w):
    k, n = w.shape
    w = f64(np.asarray(w, np.float32).astype(ml_dtypes.bfloat16)).reshape(k // 32, 32, n)
    amax = np.abs(w).max(1)
    byte = np.clip(np.where(amax > 0, np.frexp(amax)[1] - 1 + 127 - 7, 1), 1, 254)
    scaled = (w * np.exp2(127.0 - byte)[:, None, :]).reshape(k, n).astype(np.float32)
    words = np.ascontiguousarray(scaled.reshape(k // 512, 128, 4, n).transpose(0, 1, 3, 2)).astype(ml_dtypes.float8_e4m3fn).view(np.uint8)
    return words, np.ascontiguousarray(byte.astype(np.uint8).reshape(k // 512, 16, n))


def unpack_weight(words, scales):
    g, p, n, _ = words.shape
    vals = np.ascontiguousarray(words).view(ml_dtypes.float8_e4m3fn).astype(np.float64) * np.repeat(np.exp2(scales.astype(np.float64) - 127.0), 8, axis=1)[..., None]
    return vals.transpose(0, 1, 3, 2).reshape(g * 512, n)


E2M1 = np.array([0.0, 0.5, 1.0, 1.5, 2.0, 3.0, 4.0, 6.0, -0.0, -0.5, -1.0, -1.5, -2.0, -3.0, -4.0, -6.0])


def pack_fp4(w):
    k, n = w.shape
    w = f64(np.asarray(w, np.float32).astype(ml_dtypes.bfloat16)).reshape(k // 32, 32, n)
    amax = np.abs(w).max(1)
    mant, ex = np.frexp(amax / 6.0)
    byte = np.clip(np.where(amax > 0, np.where(mant > 0.5, ex, ex - 1) + 127, 1), 1, 254)
    scaled = (w * np.exp2(127.0 - byte)[:, None, :]).reshape(k, n).astype(np.float32)
    c = np.ascontiguousarray(scaled.reshape(k // 512, 128, 4, n).transpose(0, 1, 3, 2)).astype(ml_dtypes.float4_e2m1fn).view(np.uint8) & 0xF
    words = (c[..., 0::2] | (c[..., 1::2] << 4)).reshape(k // 512, 128, 2 * n)
    return np.ascontiguousarray(words), np.ascontiguousarray(byte.astype(np.uint8).reshape(k // 512, 16, n))


def unpack_fp4(words, scales):
    g, _, n = scales.shape
    words = np.ascontiguousarray(words).reshape(g, 128, n, 2)
    nib = np.empty((g, 128, n, 4), np.uint8)
    nib[..., 0::2] = words & 0xF
    nib[..., 1::2] = words >> 4
    vals = E2M1[nib] * np.repeat(np.exp2(scales.astype(np.float64) - 127.0), 8, axis=1)[..., None]
    return vals.transpose(0, 1, 3, 2).reshape(g * 512, n)


def planes(y):
    n, m = y.shape
    v = y.astype(np.float32).astype(ml_dtypes.bfloat16).astype(np.float64).reshape(n // 32, 32, m)
    top = np.abs(v).max(1)
    byte = np.clip(np.where(top > 0, np.frexp(top)[1] - 1 + 127 - 7, 1), 1, 254)
    codes = (v * np.exp2(127.0 - byte)[:, None, :]).reshape(n, m).astype(np.float32).astype(ml_dtypes.float8_e4m3fn).view(np.uint8)
    words = codes.reshape(n // 512, 128, 4, m).transpose(0, 1, 3, 2)
    return np.ascontiguousarray(words), np.ascontiguousarray(byte.astype(np.uint8).reshape(n // 512, 16, m))


def sigmoid(v):
    return 1.0 / (1.0 + np.exp(-np.maximum(v, -700.0)))


K, T, S, N, H, U = 512, 2048, 512, 512, 512, 1024


def setup_inputs():
    n = np.random.standard_normal
    s = mx_kscale(K)[:, None]
    u = mx_kscale(H)
    packed_xT = pack_weight(n((K, T)) * s)
    packed_w1 = pack_fp4(n((K, N)) / np.sqrt(K) / s)
    packed_w2 = pack_fp4(n((K, N)) / np.sqrt(K) / s)
    packed_w3 = pack_fp4(n((H, N)) / np.sqrt(H) / u[:, None])
    return {
        "x_words": packed_xT[0],
        "x_scales": packed_xT[1],
        "w1_words": packed_w1[0],
        "w1_scales": packed_w1[1],
        "w2_words": packed_w2[0],
        "w2_scales": packed_w2[1],
        "fp": (n((H, U))).astype(np.float32),
        "unit": (np.random.uniform(0.6, 1.4, (H, 1)) * u[:, None]).astype(np.float32),
        "w3_words": packed_w3[0],
        "w3_scales": packed_w3[1],
        "offs": striped(np.random.permutation(T)[:S]),
        "h1": striped(np.random.permutation(np.concatenate([np.arange(S), np.random.randint(0, S, U - S)]))),
        "h2": striped(np.random.permutation(np.concatenate([np.arange(S), np.random.randint(0, S, U - S)]))),
    }


def reference(x_words, x_scales, w1_words, w1_scales, w2_words, w2_scales, fp, unit, w3_words, w3_scales, offs, h1, h2):
    xq = unpack_weight(x_words, x_scales)[:, unstriped(offs)]
    y = unpack_fp4(w1_words, w1_scales).T @ xq
    ya = y[:, unstriped(h1)]
    m1 = -1.0 * ((np.tanh(ya) - (np.tanh(f64(fp)))) ** 2)
    yb = y[:, unstriped(h2)]
    m2 = -1.0 * ((np.tanh(yb) - (np.tanh(f64(fp)))) ** 2)
    pick_ = sigmoid(2.0 * (m1 - m2))
    yg = unpack_fp4(w2_words, w2_scales).T @ xq
    ga = yg[:, unstriped(h1)]
    hit = np.maximum(m1, m2)
    hid = f64(unit) * (pick_ * ga - (hit * yb))
    out_0 = unpack_fp4(w3_words, w3_scales).T @ mxq(hid, 0, "e4m3")
    return (out_0,) + planes(out_0)

@@ -1,0 +1,264 @@
+from contextlib import ExitStack
+
+import concourse.mybir as mybir
+from concourse.masks import make_identity
+
+F32 = mybir.dt.float32
+BF16 = mybir.dt.bfloat16
+I32 = mybir.dt.int32
+U32 = mybir.dt.uint32
+U16 = mybir.dt.uint16
+U8 = mybir.dt.uint8
+FP8X4 = mybir.dt.float8_e4m3fn_x4
+FP4X4 = mybir.dt.float4_e2m1fn_x4
+ALU = mybir.AluOpType
+ACT = mybir.ActivationFunctionType
+
+P = 128
+T, S, U = 2048, 512, 1024
+FLOPS = 2 * 512 * 512 * (2 * S + U)
+UNIT = 512
+GATHER = 256
+RANGES = (512, 256, 128, 128)
+OUT_WIDTH = 256
+SKEW = (0, 0, 1, 2, 3)
+OUT_SKEW = 4
+
+
+def tile_picked_ycuckoo_miss_po_kernel(
+    tc, x_words, x_scales, w1_words, w1_scales, w2_words, w2_scales, fp, unit, w3_words, w3_scales, offs, h1, h2,
+    out_0, out_1, out_2,
+):
+    nc = tc.nc
+    with ExitStack() as ctx:
+        keep = ctx.enter_context(tc.tile_pool(name="keep", bufs=1))
+        work = ctx.enter_context(tc.tile_pool(name="work", bufs=3))
+        wide = ctx.enter_context(tc.tile_pool(name="wide", bufs=2))
+        mm_ps = ctx.enter_context(tc.psum_pool(name="mm_ps", bufs=4))
+        tr_ps = ctx.enter_context(tc.psum_pool(name="tr_ps", bufs=2))
+
+        offs_sb = keep.tile([P, S // 16], U16)
+        h1_sb = keep.tile([P, U // 16], U16)
+        h2_sb = keep.tile([P, U // 16], U16)
+        xw = keep.tile([P, T], I32)
+        xs = keep.tile([P, T], U8)
+        xw_picked = keep.tile([P, S], U32, align_bytes=64)
+        xs_picked = keep.tile([P, S], U8, align_bytes=64)
+        unit_sb = keep.tile([P, 4], F32)
+        minus_two = keep.tile([P, 1], F32)
+        ident = keep.tile([P, P], F32)
+        ws_raw = keep.tile([P, 3 * 512], U8)
+        ww_raw = [keep.tile([P, 1024], U8, name="ww_raw%d" % i) for i in range(3)]
+        ww = [keep.tile([P, 1024], U8, name="ww%d" % i, align_bytes=64) for i in range(3)]
+        ws = [keep.tile([P, 512], U8, name="ws%d" % i, align_bytes=64) for i in range(3)]
+        ty = [keep.tile([P, S], F32, name="ty%d" % t) for t in range(4)]
+        yy = [keep.tile([P, S], F32, name="yy%d" % t) for t in range(4)]
+        yg = [keep.tile([P, S], F32, name="yg%d" % t) for t in range(4)]
+        out_codes = keep.tile([P, U], U32, align_bytes=64)
+        out_scales = keep.tile([P, U], U8, align_bytes=64)
+
+        w_words = (w1_words, w2_words, w3_words)
+        w_scales = (w1_scales, w2_scales, w3_scales)
+        fp_rows = fp.rearrange("(p t) r -> p t r", t=4)
+        out_rows = out_0.rearrange("(p t) r -> p t r", t=4)
+        code_rows = out_1[0].rearrange("p n t -> p (n t)").bitcast(I32)
+
+        units = []
+        r0 = 0
+        for c, width in enumerate(RANGES):
+            nt = UNIT // width
+            for t0 in range(0, 4, nt):
+                units.append((c, r0, width, t0, nt))
+            r0 = r0 + width
+        fp_sb = [keep.tile([P, UNIT], F32, name="fp%d" % u) for u in range(len(units))]
+
+        def load_scales(queue, dst, src):
+            for q in range(4):
+                queue.dma_start(dst[32 * q : 32 * q + 4, :].bitcast(I32), src[0][4 * q : 4 * q + 4, :].bitcast(I32))
+
+        def load_words(i):
+            nc.sync.dma_start(ww_raw[i][:].bitcast(I32), w_words[i][0].bitcast(I32))
+
+        def load_fp(u):
+            c, r0, width, t0, nt = units[u]
+            nc.sync.dma_start(fp_sb[u][:].rearrange("p (t r) -> p t r", t=nt), fp_rows[:, t0 : t0 + nt, r0 : r0 + width])
+
+        def deal(i):
+            nc.vector.tensor_copy(
+                ww[i][:].rearrange("p (t m b) -> p m t b", t=4, b=2), ww_raw[i][:].rearrange("p (m t b) -> p m t b", t=4, b=2)
+            )
+            nc.vector.tensor_copy(
+                ws[i][:].rearrange("p (t m) -> p m t", t=4),
+                ws_raw[:, 512 * i : 512 * (i + 1)].rearrange("p (m t) -> p m t", t=4),
+            )
+
+        def product(dst, i, t, codes, scales):
+            nc.tensor.matmul_mx(
+                dst, lhsT=ww[i][:, 256 * t : 256 * (t + 1)].bitcast(FP4X4), lhsT_scale=ws[i][:, P * t : P * (t + 1)],
+                rhs=codes.bitcast(FP8X4), rhs_scale=scales, start=True, stop=True,
+            )
+
+        nc.vector.memset(xs[:].bitcast(I32), 0)
+        nc.vector.memset(ws_raw[:].bitcast(I32), 0)
+        nc.sync.dma_start(offs_sb[:], offs)
+        load_words(0)
+        load_scales(nc.sync, xs, x_scales)
+        nc.sync.dma_start(xw[:], x_words[0].rearrange("p n t -> p (n t)").bitcast(I32))
+        load_scales(nc.sync, ws_raw[:, 0:512], w1_scales)
+        load_fp(0)
+        nc.sync.dma_start(h1_sb[:], h1)
+        nc.sync.dma_start(h2_sb[:], h2)
+        load_fp(1)
+        load_words(1)
+        load_scales(nc.gpsimd, ws_raw[:, 512:1024], w2_scales)
+        make_identity(nc, ident[:])
+        nc.gpsimd.memset(minus_two[:], -2.0)
+        load_scales(nc.gpsimd, ws_raw[:, 1024:1536], w3_scales)
+        nc.sync.dma_start(unit_sb[:], unit.rearrange("(p t) o -> p (t o)", t=4))
+        for u in range(2, len(units)):
+            load_fp(u)
+        load_words(2)
+
+        nc.vector.tensor_copy(xs_picked[:], xs[:].indirect(offs_sb[:]))
+        nc.vector.tensor_copy(xw_picked[:], xw[:].bitcast(U32).indirect(offs_sb[:]))
+        deal(0)
+        deal(1)
+
+        st = {}
+
+        def pieces(u):
+            c, r0, width, t0, nt = units[u]
+            n = min(width, GATHER)
+            return [
+                (t0 + k // width, slice(k, k + n), slice((r0 + k % width) // 16, (r0 + k % width + n) // 16), k % width, n)
+                for k in range(0, UNIT, n)
+            ]
+
+        def stage_fetch(u):
+            c, r0, width, t0, nt = units[u]
+            if c == 0:
+                for t in range(t0, t0 + nt):
+                    bank = mm_ps.tile([P, 512], F32, name="bank")
+                    product(bank[:], 0, t, xw_picked[:], xs_picked[:])
+                    nc.scalar.activation(ty[t][:], bank[:], ACT.Sigmoid, scale=2.0)
+                    nc.vector.tensor_copy(yy[t][:], bank[:])
+            nf = keep.tile([P, UNIT], F32, name="nf%d" % u)
+            nc.scalar.activation(nf[:], fp_sb[u][:], ACT.Sigmoid, scale=-2.0)
+            yb = work.tile([P, UNIT], F32, name="yb", bufs=5)
+            d1 = work.tile([P, UNIT], F32, name="d1")
+            for t, cols, lst, off, n in pieces(u):
+                nc.scalar.activation(yb[:, cols], yy[t][:].indirect(h2_sb[:, lst]), ACT.Copy)
+            for t, cols, lst, off, n in pieces(u):
+                nc.vector.tensor_tensor(d1[:, cols], ty[t][:].indirect(h1_sb[:, lst]), nf[:, cols], ALU.add)
+            st[u] = {"nf": nf, "yb": yb, "d1": d1}
+
+        def stage_tag(u):
+            v = st[u]
+            tb = work.tile([P, UNIT], F32, name="tb")
+            nc.scalar.activation(tb[:], v["yb"][:], ACT.Sigmoid, scale=2.0)
+            d2t = tr_ps.tile([P, UNIT], F32, name="d2t")
+            for j in range(4):
+                cols = slice(P * j, P * (j + 1))
+                nc.tensor.matmul(d2t[:, cols], lhsT=v["nf"][:, cols], rhs=ident[:], is_transpose=True, start=True, stop=False)
+                nc.tensor.matmul(d2t[:, cols], lhsT=tb[:, cols], rhs=ident[:], is_transpose=True, start=False, stop=True)
+            s1 = work.tile([P, UNIT], F32, name="s1", bufs=4)
+            nc.scalar.activation(s1[:], v["d1"][:], ACT.Square, bias=minus_two[:], scale=2.0)
+            st[u] = {"yb": v["yb"], "d2t": d2t, "s1": s1}
+
+        def stage_square(u):
+            v = st[u]
+            s2t = work.tile([P, UNIT], F32, name="s2t")
+            nc.scalar.activation(s2t[:], v["d2t"][:], ACT.Square, bias=minus_two[:], scale=2.0)
+            s2 = tr_ps.tile([P, UNIT], F32, name="s2")
+            for j in range(4):
+                cols = slice(P * j, P * (j + 1))
+                nc.tensor.transpose(s2[:, cols], s2t[:, cols], ident[:])
+            st[u] = {"yb": v["yb"], "s2": s2, "s1": v["s1"]}
+
+        def stage_choose(u):
+            c, r0, width, t0, nt = units[u]
+            v = st[u]
+            gap = work.tile([P, UNIT], F32, name="gap")
+            nc.vector.tensor_tensor(gap[:], v["s2"][:], v["s1"][:], ALU.subtract)
+            least = work.tile([P, UNIT], F32, name="least")
+            nc.vector.tensor_tensor(least[:], v["s2"][:], v["s1"][:], ALU.min)
+            pick = work.tile([P, UNIT], F32, name="pick")
+            nc.scalar.activation(pick[:], gap[:], ACT.Sigmoid, scale=2.0)
+            if c == 0:
+                for t in range(t0, t0 + nt):
+                    bank = mm_ps.tile([P, 512], F32, name="bank")
+                    product(bank[:], 1, t, xw_picked[:], xs_picked[:])
+                    nc.vector.tensor_scalar(yg[t][:], bank[:], unit_sb[:, t : t + 1], None, ALU.mult)
+            st[u] = {"yb": v["yb"], "least": least, "pick": pick}
+
+        def stage_terms(u):
+            c, r0, width, t0, nt = units[u]
+            v = st[u]
+            if t0 == 0:
+                st["terms", c] = (
+                    wide.tile([P, 4 * width], F32, name="term_a"),
+                    wide.tile([P, 4 * width], F32, name="term_b"),
+                )
+            term_a, term_b = st["terms", c]
+            for k in range(nt):
+                t = t0 + k
+                cols = slice(k * width, (k + 1) * width)
+                nc.vector.scalar_tensor_tensor(
+                    term_b[:, t * width : (t + 1) * width], v["least"][:, cols], unit_sb[:, t : t + 1], v["yb"][:, cols],
+                    ALU.mult, ALU.mult,
+                )
+            for t, cols, lst, off, n in pieces(u):
+                nc.vector.tensor_tensor(
+                    term_a[:, t * width + off : t * width + off + n], yg[t][:].indirect(h1_sb[:, lst]), v["pick"][:, cols], ALU.mult
+                )
+
+        def stage_last_product(c, r0, width, b0, n):
+            term_a, term_b = st["terms", c]
+            view = lambda x: x[:].rearrange("p (t r) -> p t r", t=4)[:, :, b0 : b0 + n].rearrange("p t (c i) -> p c t i", i=4)
+            hid = wide.tile([P, 4 * n], BF16, name="hid", align_bytes=64)
+            nc.vector.tensor_tensor(hid[:].rearrange("p (c i t) -> p c t i", i=4, t=4), view(term_a), view(term_b), ALU.add)
+            codes = wide.tile([P, n], U32, name="codes", align_bytes=64)
+            scales = wide.tile([P, n], U8, name="scales", align_bytes=64)
+            nc.vector.quantize_mx(codes[:].bitcast(FP8X4), scales[:], hid[:])
+            per_bank = 512 // n
+            banks = []
+            for t0 in range(0, 4, per_bank):
+                bank = mm_ps.tile([P, 512], F32, name="bank")
+                for k in range(per_bank):
+                    product(bank[:, k * n : (k + 1) * n], 2, t0 + k, codes[:], scales[:])
+                banks.append(bank)
+            st["banks", r0 + b0] = banks
+
+        def stage_out(r, n, last):
+            res = wide.tile([P, 4 * n], F32, name="res")
+            for k, bank in enumerate(st["banks", r]):
+                nc.scalar.copy(res[:, 512 * k : 512 * (k + 1)], bank[:])
+            nc.sync.dma_start(out_rows[:, :, r : r + n], res[:].rearrange("p (t r) -> p t r", t=4))
+            rounded = wide.tile([P, 4 * n], BF16, name="rounded", align_bytes=64)
+            dst = rounded[:].rearrange("p (c i t) -> p c t i", i=4, t=4)
+            src = res[:].rearrange("p (t c i) -> p c t i", t=4, i=4)
+            if last:
+                nc.vector.tensor_copy(dst, src)
+            else:
+                nc.scalar.copy(dst, src)
+            nc.vector.quantize_mx(out_codes[:, r : r + n].bitcast(FP8X4), out_scales[:, r : r + n], rounded[:])
+            nc.sync.dma_start(code_rows[:, r : r + n], out_codes[:, r : r + n].bitcast(I32))
+
+        stages = (stage_fetch, stage_tag, stage_square, stage_choose, stage_terms)
+        calls = []
+        for u in range(len(units)):
+            for k in range(5):
+                calls.append((u + SKEW[k], len(calls), stages[k], (u,)))
+            c, r0, width, t0, nt = units[u]
+            if t0 + nt == 4:
+                n = min(width, OUT_WIDTH)
+                for b in range(width // n):
+                    calls.append((u + SKEW[4] + b, len(calls), stage_last_product, (c, r0, width, b * n, n)))
+                    calls.append((u + OUT_SKEW + b, len(calls), stage_out, (r0 + b * n, n, u == len(units) - 1)))
+        calls.append((2.5, len(calls), deal, (2,)))
+        for key in sorted([(k[0], k[1]) for k in calls]):
+            calls[key[1]][2](*calls[key[1]][3])
+
+        for q in range(4):
+            queue = nc.sync if q % 2 == 0 else nc.scalar
+            queue.dma_start(out_2[0][4 * q : 4 * q + 4, :].bitcast(I32), out_scales[32 * q : 32 * q + 4, :].bitcast(I32))

@@ -18,11 +18,13 @@ P = 128
 T, S, U = 2048, 512, 1024
 FLOPS = 2 * 512 * 512 * (2 * S + U)
 UNIT = 512
-GATHER = 256
+GATHER = 512
+PAD = 32
 RANGES = (512, 256, 128, 128)
-OUT_WIDTH = 256
-SKEW = (0, 0, 1, 2, 3)
-OUT_SKEW = 4
+OUT_WIDTH = 128
+LATE_CHUNKS = 4
+TERM_LAG = 3
+LATE_UNITS = 2
 
 
 def tile_picked_ycuckoo_miss_po_kernel(
@@ -32,9 +34,9 @@ def tile_picked_ycuckoo_miss_po_kernel(
     nc = tc.nc
     with ExitStack() as ctx:
         keep = ctx.enter_context(tc.tile_pool(name="keep", bufs=1))
-        work = ctx.enter_context(tc.tile_pool(name="work", bufs=3))
-        wide = ctx.enter_context(tc.tile_pool(name="wide", bufs=2))
-        mm_ps = ctx.enter_context(tc.psum_pool(name="mm_ps", bufs=4))
+        work = ctx.enter_context(tc.tile_pool(name="work", bufs=4))
+        wide = ctx.enter_context(tc.tile_pool(name="wide", bufs=3))
+        psum = ctx.enter_context(tc.psum_pool(name="psum", bufs=4))
         tr_ps = ctx.enter_context(tc.psum_pool(name="tr_ps", bufs=2))
 
         offs_sb = keep.tile([P, S // 16], U16)
@@ -51,10 +53,9 @@ def tile_picked_ycuckoo_miss_po_kernel(
         ww_raw = [keep.tile([P, 1024], U8, name="ww_raw%d" % i) for i in range(3)]
         ww = [keep.tile([P, 1024], U8, name="ww%d" % i, align_bytes=64) for i in range(3)]
         ws = [keep.tile([P, 512], U8, name="ws%d" % i, align_bytes=64) for i in range(3)]
-        ty = [keep.tile([P, S], F32, name="ty%d" % t) for t in range(4)]
-        yy = [keep.tile([P, S], F32, name="yy%d" % t) for t in range(4)]
-        yg = [keep.tile([P, S], F32, name="yg%d" % t) for t in range(4)]
-        out_codes = keep.tile([P, U], U32, align_bytes=64)
+        ty = [keep.tile([P, S + PAD], F32, name="ty%d" % t) for t in range(4)]
+        yy = [keep.tile([P, S + PAD], F32, name="yy%d" % t) for t in range(4)]
+        yg = [keep.tile([P, S + PAD], F32, name="yg%d" % t) for t in range(4)]
         out_scales = keep.tile([P, U], U8, align_bytes=64)
 
         w_words = (w1_words, w2_words, w3_words)
@@ -83,14 +84,20 @@ def tile_picked_ycuckoo_miss_po_kernel(
             c, r0, width, t0, nt = units[u]
             nc.sync.dma_start(fp_sb[u][:].rearrange("p (t r) -> p t r", t=nt), fp_rows[:, t0 : t0 + nt, r0 : r0 + width])
 
-        def deal(i):
+        def deal_words(i):
             nc.vector.tensor_copy(
                 ww[i][:].rearrange("p (t m b) -> p m t b", t=4, b=2), ww_raw[i][:].rearrange("p (m t b) -> p m t b", t=4, b=2)
             )
+
+        def deal_scales(i):
             nc.vector.tensor_copy(
                 ws[i][:].rearrange("p (t m) -> p m t", t=4),
                 ws_raw[:, 512 * i : 512 * (i + 1)].rearrange("p (m t) -> p m t", t=4),
             )
+
+        def deal(i):
+            deal_words(i)
+            deal_scales(i)
 
         def product(dst, i, t, codes, scales):
             nc.tensor.matmul_mx(
@@ -99,9 +106,13 @@ def tile_picked_ycuckoo_miss_po_kernel(
             )
 
         nc.vector.memset(xs[:].bitcast(I32), 0)
+        make_identity(nc, ident[:])
+        nc.gpsimd.memset(minus_two[:], -2.0)
+        for table in ty + yy + yg:
+            nc.gpsimd.memset(table[:, S:], 0.0)
         nc.vector.memset(ws_raw[:].bitcast(I32), 0)
-        nc.sync.dma_start(offs_sb[:], offs)
         load_words(0)
+        nc.sync.dma_start(offs_sb[:], offs)
         load_scales(nc.sync, xs, x_scales)
         nc.sync.dma_start(xw[:], x_words[0].rearrange("p n t -> p (n t)").bitcast(I32))
         load_scales(nc.sync, ws_raw[:, 0:512], w1_scales)
@@ -110,19 +121,19 @@ def tile_picked_ycuckoo_miss_po_kernel(
         nc.sync.dma_start(h2_sb[:], h2)
         load_fp(1)
         load_words(1)
-        load_scales(nc.gpsimd, ws_raw[:, 512:1024], w2_scales)
-        make_identity(nc, ident[:])
-        nc.gpsimd.memset(minus_two[:], -2.0)
-        load_scales(nc.gpsimd, ws_raw[:, 1024:1536], w3_scales)
+        load_fp(2)
+        load_scales(nc.sync, ws_raw[:, 512:1024], w2_scales)
         nc.sync.dma_start(unit_sb[:], unit.rearrange("(p t) o -> p (t o)", t=4))
-        for u in range(2, len(units)):
-            load_fp(u)
+        load_fp(3)
         load_words(2)
+        load_scales(nc.sync, ws_raw[:, 1024:1536], w3_scales)
+        for u in range(4, len(units)):
+            load_fp(u)
 
+        deal_words(0)
         nc.vector.tensor_copy(xs_picked[:], xs[:].indirect(offs_sb[:]))
         nc.vector.tensor_copy(xw_picked[:], xw[:].bitcast(U32).indirect(offs_sb[:]))
-        deal(0)
-        deal(1)
+        deal_scales(0)
 
         st = {}
 
@@ -134,130 +145,189 @@ def tile_picked_ycuckoo_miss_po_kernel(
                 for k in range(0, UNIT, n)
             ]
 
-        def stage_fetch(u):
-            c, r0, width, t0, nt = units[u]
-            if c == 0:
-                for t in range(t0, t0 + nt):
-                    bank = mm_ps.tile([P, 512], F32, name="bank")
-                    product(bank[:], 0, t, xw_picked[:], xs_picked[:])
-                    nc.scalar.activation(ty[t][:], bank[:], ACT.Sigmoid, scale=2.0)
-                    nc.vector.tensor_copy(yy[t][:], bank[:])
-            nf = keep.tile([P, UNIT], F32, name="nf%d" % u)
-            nc.scalar.activation(nf[:], fp_sb[u][:], ACT.Sigmoid, scale=-2.0)
-            yb = work.tile([P, UNIT], F32, name="yb", bufs=5)
-            d1 = work.tile([P, UNIT], F32, name="d1")
-            for t, cols, lst, off, n in pieces(u):
-                nc.scalar.activation(yb[:, cols], yy[t][:].indirect(h2_sb[:, lst]), ACT.Copy)
-            for t, cols, lst, off, n in pieces(u):
-                nc.vector.tensor_tensor(d1[:, cols], ty[t][:].indirect(h1_sb[:, lst]), nf[:, cols], ALU.add)
-            st[u] = {"nf": nf, "yb": yb, "d1": d1}
-
-        def stage_tag(u):
-            v = st[u]
-            tb = work.tile([P, UNIT], F32, name="tb")
-            nc.scalar.activation(tb[:], v["yb"][:], ACT.Sigmoid, scale=2.0)
-            d2t = tr_ps.tile([P, UNIT], F32, name="d2t")
-            for j in range(4):
-                cols = slice(P * j, P * (j + 1))
-                nc.tensor.matmul(d2t[:, cols], lhsT=v["nf"][:, cols], rhs=ident[:], is_transpose=True, start=True, stop=False)
-                nc.tensor.matmul(d2t[:, cols], lhsT=tb[:, cols], rhs=ident[:], is_transpose=True, start=False, stop=True)
-            s1 = work.tile([P, UNIT], F32, name="s1", bufs=4)
-            nc.scalar.activation(s1[:], v["d1"][:], ACT.Square, bias=minus_two[:], scale=2.0)
-            st[u] = {"yb": v["yb"], "d2t": d2t, "s1": s1}
-
-        def stage_square(u):
-            v = st[u]
-            s2t = work.tile([P, UNIT], F32, name="s2t")
-            nc.scalar.activation(s2t[:], v["d2t"][:], ACT.Square, bias=minus_two[:], scale=2.0)
-            s2 = tr_ps.tile([P, UNIT], F32, name="s2")
-            for j in range(4):
-                cols = slice(P * j, P * (j + 1))
-                nc.tensor.transpose(s2[:, cols], s2t[:, cols], ident[:])
-            st[u] = {"yb": v["yb"], "s2": s2, "s1": v["s1"]}
-
-        def stage_choose(u):
-            c, r0, width, t0, nt = units[u]
-            v = st[u]
-            gap = work.tile([P, UNIT], F32, name="gap")
-            nc.vector.tensor_tensor(gap[:], v["s2"][:], v["s1"][:], ALU.subtract)
-            least = work.tile([P, UNIT], F32, name="least")
-            nc.vector.tensor_tensor(least[:], v["s2"][:], v["s1"][:], ALU.min)
-            pick = work.tile([P, UNIT], F32, name="pick")
-            nc.scalar.activation(pick[:], gap[:], ACT.Sigmoid, scale=2.0)
-            if c == 0:
-                for t in range(t0, t0 + nt):
-                    bank = mm_ps.tile([P, 512], F32, name="bank")
-                    product(bank[:], 1, t, xw_picked[:], xs_picked[:])
-                    nc.vector.tensor_scalar(yg[t][:], bank[:], unit_sb[:, t : t + 1], None, ALU.mult)
-            st[u] = {"yb": v["yb"], "least": least, "pick": pick}
-
-        def stage_terms(u):
-            c, r0, width, t0, nt = units[u]
-            v = st[u]
-            if t0 == 0:
-                st["terms", c] = (
-                    wide.tile([P, 4 * width], F32, name="term_a"),
-                    wide.tile([P, 4 * width], F32, name="term_b"),
-                )
-            term_a, term_b = st["terms", c]
-            for k in range(nt):
-                t = t0 + k
-                cols = slice(k * width, (k + 1) * width)
-                nc.vector.scalar_tensor_tensor(
-                    term_b[:, t * width : (t + 1) * width], v["least"][:, cols], unit_sb[:, t : t + 1], v["yb"][:, cols],
-                    ALU.mult, ALU.mult,
-                )
-            for t, cols, lst, off, n in pieces(u):
-                nc.vector.tensor_tensor(
-                    term_a[:, t * width + off : t * width + off + n], yg[t][:].indirect(h1_sb[:, lst]), v["pick"][:, cols], ALU.mult
-                )
-
-        def stage_last_product(c, r0, width, b0, n):
-            term_a, term_b = st["terms", c]
-            view = lambda x: x[:].rearrange("p (t r) -> p t r", t=4)[:, :, b0 : b0 + n].rearrange("p t (c i) -> p c t i", i=4)
-            hid = wide.tile([P, 4 * n], BF16, name="hid", align_bytes=64)
-            nc.vector.tensor_tensor(hid[:].rearrange("p (c i t) -> p c t i", i=4, t=4), view(term_a), view(term_b), ALU.add)
-            codes = wide.tile([P, n], U32, name="codes", align_bytes=64)
-            scales = wide.tile([P, n], U8, name="scales", align_bytes=64)
-            nc.vector.quantize_mx(codes[:].bitcast(FP8X4), scales[:], hid[:])
-            per_bank = 512 // n
-            banks = []
-            for t0 in range(0, 4, per_bank):
-                bank = mm_ps.tile([P, 512], F32, name="bank")
-                for k in range(per_bank):
-                    product(bank[:, k * n : (k + 1) * n], 2, t0 + k, codes[:], scales[:])
-                banks.append(bank)
-            st["banks", r0 + b0] = banks
-
-        def stage_out(r, n, last):
-            res = wide.tile([P, 4 * n], F32, name="res")
-            for k, bank in enumerate(st["banks", r]):
-                nc.scalar.copy(res[:, 512 * k : 512 * (k + 1)], bank[:])
-            nc.sync.dma_start(out_rows[:, :, r : r + n], res[:].rearrange("p (t r) -> p t r", t=4))
-            rounded = wide.tile([P, 4 * n], BF16, name="rounded", align_bytes=64)
-            dst = rounded[:].rearrange("p (c i t) -> p c t i", i=4, t=4)
-            src = res[:].rearrange("p (t c i) -> p c t i", t=4, i=4)
-            if last:
-                nc.vector.tensor_copy(dst, src)
-            else:
-                nc.scalar.copy(dst, src)
-            nc.vector.quantize_mx(out_codes[:, r : r + n].bitcast(FP8X4), out_scales[:, r : r + n], rounded[:])
-            nc.sync.dma_start(code_rows[:, r : r + n], out_codes[:, r : r + n].bitcast(I32))
-
-        stages = (stage_fetch, stage_tag, stage_square, stage_choose, stage_terms)
-        calls = []
-        for u in range(len(units)):
-            for k in range(5):
-                calls.append((u + SKEW[k], len(calls), stages[k], (u,)))
-            c, r0, width, t0, nt = units[u]
+        n_units = len(units)
+        chunks = []
+        for u, (c, r0, width, t0, nt) in enumerate(units):
             if t0 + nt == 4:
-                n = min(width, OUT_WIDTH)
-                for b in range(width // n):
-                    calls.append((u + SKEW[4] + b, len(calls), stage_last_product, (c, r0, width, b * n, n)))
-                    calls.append((u + OUT_SKEW + b, len(calls), stage_out, (r0 + b * n, n, u == len(units) - 1)))
-        calls.append((2.5, len(calls), deal, (2,)))
-        for key in sorted([(k[0], k[1]) for k in calls]):
-            calls[key[1]][2](*calls[key[1]][3])
+                for b0 in range(0, width, OUT_WIDTH):
+                    step = u + TERM_LAG + 1 + (1 if u < n_units - 1 else 0)
+                    if chunks:
+                        step = max(step, chunks[-1][4] + (1 if u < n_units - 1 else 0))
+                    chunks.append((c, r0, width, b0, step))
+
+        def new(name, u, pool=work, dtype=F32, width=UNIT, bufs=None):
+            st[name, u] = pool.tile([P, width], dtype, name=name, align_bytes=64, bufs=bufs)
+            return st[name, u]
+
+        def live(u):
+            return 0 <= u < n_units
+
+        def tag_tables(u):
+            if live(u) and units[u][0] == 0:
+                for t in range(units[u][3], units[u][3] + units[u][4]):
+                    bank = psum.tile([P, 512], F32, name="bank")
+                    product(bank[:], 0, t, xw_picked[:], xs_picked[:])
+                    nc.scalar.activation(ty[t][:, 0:S], bank[:], ACT.Sigmoid, scale=2.0)
+                    nc.vector.tensor_copy(yy[t][:, 0:S], bank[:])
+
+        def value_tables(u):
+            if u in (0, 1):
+                deal(u + 1)
+            if live(u) and units[u][0] == 0:
+                for t in range(units[u][3], units[u][3] + units[u][4]):
+                    bank = psum.tile([P, 512], F32, name="bank")
+                    product(bank[:], 1, t, xw_picked[:], xs_picked[:])
+                    nc.scalar.activation(yg[t][:, 0:S], bank[:], ACT.Copy, scale=unit_sb[:, t : t + 1])
+
+        def fingerprint(u):
+            if live(u):
+                nc.scalar.activation(new("nf", u, bufs=8)[:], fp_sb[u][:], ACT.Sigmoid, scale=-2.0)
+
+        def fetch_second(u):
+            if live(u):
+                yb = new("yb", u, bufs=6)
+                for t, cols, lst, off, n in pieces(u):
+                    nc.scalar.activation(yb[:, cols], yy[t][:].indirect(h2_sb[:, lst]), ACT.Copy)
+
+        def first_difference(u):
+            if live(u):
+                d1 = new("d1", u)
+                for t, cols, lst, off, n in pieces(u):
+                    nc.vector.tensor_tensor(d1[:, cols], ty[t][:].indirect(h1_sb[:, lst]), st["nf", u][:, cols], ALU.add)
+
+        def second_difference(u):
+            if live(u):
+                tb = new("tb", u)
+                nc.scalar.activation(tb[:], st["yb", u][:], ACT.Sigmoid, scale=2.0)
+                d2t = tr_ps.tile([P, UNIT], F32, name="d2t")
+                st["d2t", u] = d2t
+                for j in range(4):
+                    cols = slice(P * j, P * (j + 1))
+                    nc.tensor.matmul(d2t[:, cols], lhsT=st["nf", u][:, cols], rhs=ident[:], is_transpose=True, start=True, stop=False)
+                    nc.tensor.matmul(d2t[:, cols], lhsT=tb[:, cols], rhs=ident[:], is_transpose=True, start=False, stop=True)
+
+        def first_square(u):
+            if live(u):
+                nc.scalar.activation(new("s1", u)[:], st["d1", u][:], ACT.Square, bias=minus_two[:], scale=2.0)
+
+        def second_square(u):
+            if live(u):
+                s2t = new("s2t", u)
+                nc.scalar.activation(s2t[:], st["d2t", u][:], ACT.Square, bias=minus_two[:], scale=2.0)
+                s2 = tr_ps.tile([P, UNIT], F32, name="s2")
+                st["s2", u] = s2
+                for j in range(4):
+                    cols = slice(P * j, P * (j + 1))
+                    nc.tensor.transpose(s2[:, cols], s2t[:, cols], ident[:])
+
+        def fetch_values(u):
+            if n_units - LATE_UNITS <= u < n_units:
+                ga = new("ga", u)
+                for t, cols, lst, off, n in pieces(u):
+                    nc.scalar.activation(ga[:, cols], yg[t][:].indirect(h1_sb[:, lst]), ACT.Copy)
+
+        def gap_of(u):
+            if live(u):
+                nc.vector.tensor_tensor(new("gap", u)[:], st["s2", u][:], st["s1", u][:], ALU.subtract)
+
+        def least_of(u):
+            if live(u):
+                nc.vector.tensor_tensor(new("least", u)[:], st["s2", u][:], st["s1", u][:], ALU.min)
+
+        def pick_of(u):
+            if live(u):
+                nc.scalar.activation(new("pick", u)[:], st["gap", u][:], ACT.Sigmoid, scale=2.0)
+
+        def miss_term(u):
+            if live(u):
+                c, r0, width, t0, nt = units[u]
+                if t0 == 0:
+                    new("miss", c, pool=wide, width=4 * width)
+                for k in range(nt):
+                    t = t0 + k
+                    cols = slice(k * width, (k + 1) * width)
+                    nc.vector.scalar_tensor_tensor(
+                        st["miss", c][:, t * width : (t + 1) * width], st["least", u][:, cols], unit_sb[:, t : t + 1],
+                        st["yb", u][:, cols], ALU.mult, ALU.mult,
+                    )
+
+        def hit_term(u):
+            if live(u):
+                c, r0, width, t0, nt = units[u]
+                if t0 == 0:
+                    new("hit", c, pool=wide, width=4 * width)
+                hit = st["hit", c]
+                if u >= n_units - LATE_UNITS:
+                    nc.vector.tensor_tensor(hit[:, t0 * width : (t0 + nt) * width], st["ga", u][:], st["pick", u][:], ALU.mult)
+                else:
+                    for t, cols, lst, off, n in pieces(u):
+                        nc.vector.tensor_tensor(
+                            hit[:, t * width + off : t * width + off + n], yg[t][:].indirect(h1_sb[:, lst]), st["pick", u][:, cols], ALU.mult
+                        )
+
+        def each_chunk(k, action):
+            for j in range(len(chunks)):
+                if chunks[j][4] == k:
+                    action(j)
+
+        def add_terms(j):
+            c, r0, width, b0, step = chunks[j]
+            view = lambda x: x[:].rearrange("p (t r) -> p t r", t=4)[:, :, b0 : b0 + OUT_WIDTH].rearrange("p t (c i) -> p c t i", i=4)
+            hid = new("hid", j, pool=wide, dtype=BF16)
+            nc.vector.tensor_tensor(hid[:].rearrange("p (c i t) -> p c t i", i=4, t=4), view(st["hit", c]), view(st["miss", c]), ALU.add)
+
+        def last_product(j):
+            codes = new("codes", j, pool=wide, dtype=U32, width=OUT_WIDTH)
+            scales = new("scales", j, pool=wide, dtype=U8, width=OUT_WIDTH)
+            nc.vector.quantize_mx(codes[:].bitcast(FP8X4), scales[:], st["hid", j][:])
+            bank = psum.tile([P, 512], F32, name="bank")
+            for t in range(4):
+                product(bank[:, t * OUT_WIDTH : (t + 1) * OUT_WIDTH], 2, t, codes[:], scales[:])
+            st["bank", j] = bank
+
+        def leave_bank(j):
+            c, r0, width, b0, step = chunks[j]
+            r = r0 + b0
+            bank = st["bank", j]
+            res = new("res", j, pool=wide, bufs=8)
+            nc.scalar.copy(res[:], bank[:])
+            nc.sync.dma_start(out_rows[:, :, r : r + OUT_WIDTH], res[:].rearrange("p (t r) -> p t r", t=4))
+            if j < len(chunks) - LATE_CHUNKS:
+                rounded = new("rounded", j, pool=wide, dtype=BF16)
+                nc.scalar.copy(rounded[:].rearrange("p (c t) -> p c t", t=4), bank[:].rearrange("p (t c) -> p c t", t=4))
+
+        def quantise_result(j):
+            c, r0, width, b0, step = chunks[j]
+            r = r0 + b0
+            if j >= len(chunks) - LATE_CHUNKS:
+                nc.vector.tensor_copy(
+                    new("rounded", j, pool=wide, dtype=BF16)[:].rearrange("p (c i t) -> p c t i", i=4, t=4),
+                    st["res", j][:].rearrange("p (t c i) -> p c t i", t=4, i=4),
+                )
+            out_codes = new("out_codes", j, pool=wide, dtype=U32, width=OUT_WIDTH, bufs=8)
+            nc.vector.quantize_mx(out_codes[:].bitcast(FP8X4), out_scales[:, r : r + OUT_WIDTH], st["rounded", j][:])
+            nc.sync.dma_start(code_rows[:, r : r + OUT_WIDTH], out_codes[:].bitcast(I32))
+
+        fingerprint(0)
+        for k in range(chunks[-1][4] + 2):
+            tag_tables(k)
+            gap_of(k - 2)
+            second_square(k - 1)
+            least_of(k - 2)
+            each_chunk(k, add_terms)
+            fetch_second(k)
+            first_difference(k)
+            each_chunk(k, last_product)
+            pick_of(k - 2)
+            value_tables(k - 1)
+            second_difference(k)
+            miss_term(k - TERM_LAG)
+            first_square(k)
+            each_chunk(k - 1, quantise_result)
+            hit_term(k - TERM_LAG)
+            fingerprint(k + 1)
+            fetch_values(k - 1)
+            each_chunk(k, leave_bank)
 
         for q in range(4):
             queue = nc.sync if q % 2 == 0 else nc.scalar

@@ -15,16 +15,20 @@ ALU = mybir.AluOpType
 ACT = mybir.ActivationFunctionType
 
 P = 128
-T, S, U = 2048, 512, 1024
-FLOPS = 2 * 512 * 512 * (2 * S + U)
-UNIT = 512
-GATHER = 512
-PAD = 32
-RANGES = (512, 256, 128, 128)
-OUT_WIDTH = 128
-LATE_CHUNKS = 4
+ROW_TILES = 4
+TABLE = 2048
+PICKED = 512
+QUERIES = 1024
+FEATURES = 512
+FLOPS = 2 * 512 * FEATURES * (2 * PICKED + QUERIES)
+
+PIECE = 512
+CHUNK = 256
+GATHER = 256
+RANGES = (256, 512, 128, 128)
+LATE_PIECES = 2
+LATE_CHUNKS = 2
 TERM_LAG = 3
-LATE_UNITS = 2
 
 
 def tile_picked_ycuckoo_miss_po_kernel(
@@ -36,98 +40,104 @@ def tile_picked_ycuckoo_miss_po_kernel(
         keep = ctx.enter_context(tc.tile_pool(name="keep", bufs=1))
         work = ctx.enter_context(tc.tile_pool(name="work", bufs=4))
         wide = ctx.enter_context(tc.tile_pool(name="wide", bufs=3))
-        psum = ctx.enter_context(tc.psum_pool(name="psum", bufs=4))
-        tr_ps = ctx.enter_context(tc.psum_pool(name="tr_ps", bufs=2))
+        mx_banks = ctx.enter_context(tc.psum_pool(name="mx_banks", bufs=4))
+        turn_banks = ctx.enter_context(tc.psum_pool(name="turn_banks", bufs=2))
 
-        offs_sb = keep.tile([P, S // 16], U16)
-        h1_sb = keep.tile([P, U // 16], U16)
-        h2_sb = keep.tile([P, U // 16], U16)
-        xw = keep.tile([P, T], I32)
-        xs = keep.tile([P, T], U8)
-        xw_picked = keep.tile([P, S], U32, align_bytes=64)
-        xs_picked = keep.tile([P, S], U8, align_bytes=64)
-        unit_sb = keep.tile([P, 4], F32)
+        offs_sb = keep.tile([P, PICKED // 16], U16)
+        h1_sb = keep.tile([P, QUERIES // 16], U16)
+        h2_sb = keep.tile([P, QUERIES // 16], U16)
+        xw = keep.tile([P, TABLE], I32)
+        xs = keep.tile([P, TABLE], U8)
+        xw_picked = keep.tile([P, PICKED], U32, align_bytes=64)
+        xs_picked = keep.tile([P, PICKED], U8, align_bytes=64)
+        unit_sb = keep.tile([P, ROW_TILES], F32)
         minus_two = keep.tile([P, 1], F32)
         ident = keep.tile([P, P], F32)
-        ws_raw = keep.tile([P, 3 * 512], U8)
-        ww_raw = [keep.tile([P, 1024], U8, name="ww_raw%d" % i) for i in range(3)]
-        ww = [keep.tile([P, 1024], U8, name="ww%d" % i, align_bytes=64) for i in range(3)]
-        ws = [keep.tile([P, 512], U8, name="ws%d" % i, align_bytes=64) for i in range(3)]
-        ty = [keep.tile([P, S + PAD], F32, name="ty%d" % t) for t in range(4)]
-        yy = [keep.tile([P, S + PAD], F32, name="yy%d" % t) for t in range(4)]
-        yg = [keep.tile([P, S + PAD], F32, name="yg%d" % t) for t in range(4)]
-        out_scales = keep.tile([P, U], U8, align_bytes=64)
+        ws_raw = keep.tile([P, 3 * FEATURES], U8)
+        ww_raw = [keep.tile([P, 2 * FEATURES], U8, name="ww_raw%d" % i) for i in range(3)]
+        ww = [keep.tile([P, 2 * FEATURES], U8, name="ww%d" % i, align_bytes=64) for i in range(3)]
+        ws = [keep.tile([P, FEATURES], U8, name="ws%d" % i, align_bytes=64) for i in range(3)]
+        tags = [keep.tile([P, PICKED], F32, name="tags%d" % t) for t in range(ROW_TILES)]
+        ys = [keep.tile([P, PICKED], F32, name="ys%d" % t) for t in range(ROW_TILES)]
+        values = [keep.tile([P, PICKED], F32, name="values%d" % t) for t in range(ROW_TILES)]
+        out_scales = keep.tile([P, QUERIES], U8, align_bytes=64)
 
         w_words = (w1_words, w2_words, w3_words)
         w_scales = (w1_scales, w2_scales, w3_scales)
-        fp_rows = fp.rearrange("(p t) r -> p t r", t=4)
-        out_rows = out_0.rearrange("(p t) r -> p t r", t=4)
+        fp_rows = fp.rearrange("(p t) r -> p t r", t=ROW_TILES)
+        out_rows = out_0.rearrange("(p t) r -> p t r", t=ROW_TILES)
         code_rows = out_1[0].rearrange("p n t -> p (n t)").bitcast(I32)
 
-        units = []
-        r0 = 0
+        pieces = []
         for c, width in enumerate(RANGES):
-            nt = UNIT // width
-            for t0 in range(0, 4, nt):
-                units.append((c, r0, width, t0, nt))
-            r0 = r0 + width
-        fp_sb = [keep.tile([P, UNIT], F32, name="fp%d" % u) for u in range(len(units))]
+            nt = PIECE // width
+            pieces.extend([(c, sum(RANGES[:c]), width, t0, nt) for t0 in range(0, ROW_TILES, nt)])
+        n_pieces = len(pieces)
+        chunks = []
+        for u, (c, r0, width, t0, nt) in enumerate(pieces):
+            if t0 + nt == ROW_TILES:
+                apart = 0 if u == n_pieces - 1 else 1
+                for b0 in range(0, width, CHUNK):
+                    step = u + TERM_LAG + 1 + apart
+                    if chunks:
+                        step = max(step, chunks[-1][3] + apart)
+                    chunks.append((c, r0, b0, step, min(width, CHUNK)))
+        fp_sb = [keep.tile([P, PIECE], F32, name="fp%d" % u) for u in range(n_pieces)]
 
-        def load_scales(queue, dst, src):
+        def load_scales(dst, src):
             for q in range(4):
-                queue.dma_start(dst[32 * q : 32 * q + 4, :].bitcast(I32), src[0][4 * q : 4 * q + 4, :].bitcast(I32))
+                nc.sync.dma_start(dst[32 * q : 32 * q + 4, :].bitcast(I32), src[0][4 * q : 4 * q + 4, :].bitcast(I32))
 
-        def load_words(i):
+        def load_weight_scales(i):
+            load_scales(ws_raw[:, FEATURES * i : FEATURES * (i + 1)], w_scales[i])
+
+        def load_weight_words(i):
             nc.sync.dma_start(ww_raw[i][:].bitcast(I32), w_words[i][0].bitcast(I32))
 
         def load_fp(u):
-            c, r0, width, t0, nt = units[u]
+            c, r0, width, t0, nt = pieces[u]
             nc.sync.dma_start(fp_sb[u][:].rearrange("p (t r) -> p t r", t=nt), fp_rows[:, t0 : t0 + nt, r0 : r0 + width])
 
         def deal_words(i):
             nc.vector.tensor_copy(
-                ww[i][:].rearrange("p (t m b) -> p m t b", t=4, b=2), ww_raw[i][:].rearrange("p (m t b) -> p m t b", t=4, b=2)
+                ww[i][:].rearrange("p (t m b) -> p t m b", t=ROW_TILES, b=2),
+                ww_raw[i][:].rearrange("p (m t b) -> p t m b", t=ROW_TILES, b=2),
             )
 
         def deal_scales(i):
             nc.vector.tensor_copy(
-                ws[i][:].rearrange("p (t m) -> p m t", t=4),
-                ws_raw[:, 512 * i : 512 * (i + 1)].rearrange("p (m t) -> p m t", t=4),
+                ws[i][:].rearrange("p (t m) -> p t m", t=ROW_TILES),
+                ws_raw[:, FEATURES * i : FEATURES * (i + 1)].rearrange("p (m t) -> p t m", t=ROW_TILES),
             )
-
-        def deal(i):
-            deal_words(i)
-            deal_scales(i)
 
         def product(dst, i, t, codes, scales):
             nc.tensor.matmul_mx(
-                dst, lhsT=ww[i][:, 256 * t : 256 * (t + 1)].bitcast(FP4X4), lhsT_scale=ws[i][:, P * t : P * (t + 1)],
+                dst, lhsT=ww[i][:, 2 * P * t : 2 * P * (t + 1)].bitcast(FP4X4), lhsT_scale=ws[i][:, P * t : P * (t + 1)],
                 rhs=codes.bitcast(FP8X4), rhs_scale=scales, start=True, stop=True,
             )
 
         nc.vector.memset(xs[:].bitcast(I32), 0)
         make_identity(nc, ident[:])
         nc.gpsimd.memset(minus_two[:], -2.0)
-        for table in ty + yy + yg:
-            nc.gpsimd.memset(table[:, S:], 0.0)
         nc.vector.memset(ws_raw[:].bitcast(I32), 0)
-        load_words(0)
+
         nc.sync.dma_start(offs_sb[:], offs)
-        load_scales(nc.sync, xs, x_scales)
+        load_weight_words(0)
+        load_scales(xs, x_scales)
         nc.sync.dma_start(xw[:], x_words[0].rearrange("p n t -> p (n t)").bitcast(I32))
-        load_scales(nc.sync, ws_raw[:, 0:512], w1_scales)
+        load_weight_scales(0)
         load_fp(0)
         nc.sync.dma_start(h1_sb[:], h1)
         nc.sync.dma_start(h2_sb[:], h2)
         load_fp(1)
-        load_words(1)
+        load_weight_words(1)
         load_fp(2)
-        load_scales(nc.sync, ws_raw[:, 512:1024], w2_scales)
-        nc.sync.dma_start(unit_sb[:], unit.rearrange("(p t) o -> p (t o)", t=4))
+        load_weight_scales(1)
+        nc.sync.dma_start(unit_sb[:], unit.rearrange("(p t) o -> p (t o)", t=ROW_TILES))
         load_fp(3)
-        load_words(2)
-        load_scales(nc.sync, ws_raw[:, 1024:1536], w3_scales)
-        for u in range(4, len(units)):
+        load_weight_words(2)
+        load_weight_scales(2)
+        for u in range(4, n_pieces):
             load_fp(u)
 
         deal_words(0)
@@ -135,199 +145,203 @@ def tile_picked_ycuckoo_miss_po_kernel(
         nc.vector.tensor_copy(xw_picked[:], xw[:].bitcast(U32).indirect(offs_sb[:]))
         deal_scales(0)
 
-        st = {}
+        made = {}
 
-        def pieces(u):
-            c, r0, width, t0, nt = units[u]
-            n = min(width, GATHER)
-            return [
-                (t0 + k // width, slice(k, k + n), slice((r0 + k % width) // 16, (r0 + k % width + n) // 16), k % width, n)
-                for k in range(0, UNIT, n)
-            ]
-
-        n_units = len(units)
-        chunks = []
-        for u, (c, r0, width, t0, nt) in enumerate(units):
-            if t0 + nt == 4:
-                for b0 in range(0, width, OUT_WIDTH):
-                    step = u + TERM_LAG + 1 + (1 if u < n_units - 1 else 0)
-                    if chunks:
-                        step = max(step, chunks[-1][4] + (1 if u < n_units - 1 else 0))
-                    chunks.append((c, r0, width, b0, step))
-
-        def new(name, u, pool=work, dtype=F32, width=UNIT, bufs=None):
-            st[name, u] = pool.tile([P, width], dtype, name=name, align_bytes=64, bufs=bufs)
-            return st[name, u]
+        def new(name, key, pool=work, dtype=F32, width=PIECE, bufs=None):
+            made[name, key] = pool.tile([P, width], dtype, name=name, align_bytes=64, bufs=bufs)
+            return made[name, key]
 
         def live(u):
-            return 0 <= u < n_units
+            return 0 <= u < n_pieces
+
+        def row_tiles_first_met(u):
+            return range(pieces[u][3], pieces[u][3] + pieces[u][4]) if live(u) and pieces[u][0] == 0 else ()
+
+        def gathers(u):
+            c, r0, width, t0, nt = pieces[u]
+            n = min(width, GATHER)
+            return [
+                (
+                    t0 + k // width,
+                    slice(k, k + n),
+                    slice((r0 + k % width) // 16, (r0 + k % width + n) // 16),
+                    slice(t0 * width + k, t0 * width + k + n),
+                )
+                for k in range(0, PIECE, n)
+            ]
 
         def tag_tables(u):
-            if live(u) and units[u][0] == 0:
-                for t in range(units[u][3], units[u][3] + units[u][4]):
-                    bank = psum.tile([P, 512], F32, name="bank")
-                    product(bank[:], 0, t, xw_picked[:], xs_picked[:])
-                    nc.scalar.activation(ty[t][:, 0:S], bank[:], ACT.Sigmoid, scale=2.0)
-                    nc.vector.tensor_copy(yy[t][:, 0:S], bank[:])
+            for t in row_tiles_first_met(u):
+                bank = mx_banks.tile([P, PIECE], F32, name="bank")
+                product(bank[:], 0, t, xw_picked[:], xs_picked[:])
+                nc.scalar.activation(tags[t][:], bank[:], ACT.Sigmoid, scale=2.0)
+                nc.vector.tensor_copy(ys[t][:], bank[:])
 
         def value_tables(u):
             if u in (0, 1):
-                deal(u + 1)
-            if live(u) and units[u][0] == 0:
-                for t in range(units[u][3], units[u][3] + units[u][4]):
-                    bank = psum.tile([P, 512], F32, name="bank")
-                    product(bank[:], 1, t, xw_picked[:], xs_picked[:])
-                    nc.scalar.activation(yg[t][:, 0:S], bank[:], ACT.Copy, scale=unit_sb[:, t : t + 1])
+                deal_words(u + 1)
+                deal_scales(u + 1)
+            for t in row_tiles_first_met(u):
+                bank = mx_banks.tile([P, PIECE], F32, name="bank")
+                product(bank[:], 1, t, xw_picked[:], xs_picked[:])
+                nc.scalar.activation(values[t][:], bank[:], ACT.Copy, scale=unit_sb[:, t : t + 1])
 
         def fingerprint(u):
             if live(u):
-                nc.scalar.activation(new("nf", u, bufs=8)[:], fp_sb[u][:], ACT.Sigmoid, scale=-2.0)
+                nc.scalar.activation(new("nf", u, bufs=n_pieces)[:], fp_sb[u][:], ACT.Sigmoid, scale=-2.0)
 
         def fetch_second(u):
             if live(u):
                 yb = new("yb", u, bufs=6)
-                for t, cols, lst, off, n in pieces(u):
-                    nc.scalar.activation(yb[:, cols], yy[t][:].indirect(h2_sb[:, lst]), ACT.Copy)
+                for t, cols, lst, span in gathers(u):
+                    nc.scalar.activation(yb[:, cols], ys[t][:].indirect(h2_sb[:, lst]), ACT.Copy)
 
-        def first_difference(u):
+        def first_sum(u):
             if live(u):
                 d1 = new("d1", u)
-                for t, cols, lst, off, n in pieces(u):
-                    nc.vector.tensor_tensor(d1[:, cols], ty[t][:].indirect(h1_sb[:, lst]), st["nf", u][:, cols], ALU.add)
+                for t, cols, lst, span in gathers(u):
+                    nc.vector.tensor_tensor(d1[:, cols], tags[t][:].indirect(h1_sb[:, lst]), made["nf", u][:, cols], ALU.add)
 
-        def second_difference(u):
+        def second_sum(u):
             if live(u):
                 tb = new("tb", u)
-                nc.scalar.activation(tb[:], st["yb", u][:], ACT.Sigmoid, scale=2.0)
-                d2t = tr_ps.tile([P, UNIT], F32, name="d2t")
-                st["d2t", u] = d2t
-                for j in range(4):
+                nc.scalar.activation(tb[:], made["yb", u][:], ACT.Sigmoid, scale=2.0)
+                d2t = turn_banks.tile([P, PIECE], F32, name="d2t")
+                made["d2t", u] = d2t
+                for j in range(PIECE // P):
                     cols = slice(P * j, P * (j + 1))
-                    nc.tensor.matmul(d2t[:, cols], lhsT=st["nf", u][:, cols], rhs=ident[:], is_transpose=True, start=True, stop=False)
+                    nc.tensor.matmul(d2t[:, cols], lhsT=made["nf", u][:, cols], rhs=ident[:], is_transpose=True, start=True, stop=False)
                     nc.tensor.matmul(d2t[:, cols], lhsT=tb[:, cols], rhs=ident[:], is_transpose=True, start=False, stop=True)
 
         def first_square(u):
             if live(u):
-                nc.scalar.activation(new("s1", u)[:], st["d1", u][:], ACT.Square, bias=minus_two[:], scale=2.0)
+                nc.scalar.activation(new("s1", u)[:], made["d1", u][:], ACT.Square, bias=minus_two[:], scale=2.0)
 
         def second_square(u):
             if live(u):
                 s2t = new("s2t", u)
-                nc.scalar.activation(s2t[:], st["d2t", u][:], ACT.Square, bias=minus_two[:], scale=2.0)
-                s2 = tr_ps.tile([P, UNIT], F32, name="s2")
-                st["s2", u] = s2
-                for j in range(4):
+                nc.scalar.activation(s2t[:], made["d2t", u][:], ACT.Square, bias=minus_two[:], scale=2.0)
+                s2 = turn_banks.tile([P, PIECE], F32, name="s2")
+                made["s2", u] = s2
+                for j in range(PIECE // P):
                     cols = slice(P * j, P * (j + 1))
                     nc.tensor.transpose(s2[:, cols], s2t[:, cols], ident[:])
 
         def fetch_values(u):
-            if n_units - LATE_UNITS <= u < n_units:
+            if n_pieces - LATE_PIECES <= u < n_pieces:
                 ga = new("ga", u)
-                for t, cols, lst, off, n in pieces(u):
-                    nc.scalar.activation(ga[:, cols], yg[t][:].indirect(h1_sb[:, lst]), ACT.Copy)
+                for t, cols, lst, span in gathers(u):
+                    nc.scalar.activation(ga[:, cols], values[t][:].indirect(h1_sb[:, lst]), ACT.Copy)
 
         def gap_of(u):
             if live(u):
-                nc.vector.tensor_tensor(new("gap", u)[:], st["s2", u][:], st["s1", u][:], ALU.subtract)
+                nc.vector.tensor_tensor(new("gap", u)[:], made["s2", u][:], made["s1", u][:], ALU.subtract)
 
         def least_of(u):
             if live(u):
-                nc.vector.tensor_tensor(new("least", u)[:], st["s2", u][:], st["s1", u][:], ALU.min)
+                nc.vector.tensor_tensor(new("least", u)[:], made["s2", u][:], made["s1", u][:], ALU.min)
 
         def pick_of(u):
             if live(u):
-                nc.scalar.activation(new("pick", u)[:], st["gap", u][:], ACT.Sigmoid, scale=2.0)
+                nc.scalar.activation(new("pick", u)[:], made["gap", u][:], ACT.Sigmoid, scale=2.0)
 
         def miss_term(u):
             if live(u):
-                c, r0, width, t0, nt = units[u]
+                c, r0, width, t0, nt = pieces[u]
                 if t0 == 0:
-                    new("miss", c, pool=wide, width=4 * width)
+                    new("miss", c, pool=wide, width=ROW_TILES * width)
                 for k in range(nt):
                     t = t0 + k
                     cols = slice(k * width, (k + 1) * width)
                     nc.vector.scalar_tensor_tensor(
-                        st["miss", c][:, t * width : (t + 1) * width], st["least", u][:, cols], unit_sb[:, t : t + 1],
-                        st["yb", u][:, cols], ALU.mult, ALU.mult,
+                        made["miss", c][:, t * width : (t + 1) * width], made["least", u][:, cols], unit_sb[:, t : t + 1],
+                        made["yb", u][:, cols], ALU.mult, ALU.mult,
                     )
 
-        def hit_term(u):
+        def pick_term(u):
             if live(u):
-                c, r0, width, t0, nt = units[u]
+                c, r0, width, t0, nt = pieces[u]
                 if t0 == 0:
-                    new("hit", c, pool=wide, width=4 * width)
-                hit = st["hit", c]
-                if u >= n_units - LATE_UNITS:
-                    nc.vector.tensor_tensor(hit[:, t0 * width : (t0 + nt) * width], st["ga", u][:], st["pick", u][:], ALU.mult)
+                    new("picked", c, pool=wide, width=ROW_TILES * width)
+                picked = made["picked", c]
+                if u >= n_pieces - LATE_PIECES:
+                    nc.vector.tensor_tensor(picked[:, t0 * width : (t0 + nt) * width], made["ga", u][:], made["pick", u][:], ALU.mult)
                 else:
-                    for t, cols, lst, off, n in pieces(u):
-                        nc.vector.tensor_tensor(
-                            hit[:, t * width + off : t * width + off + n], yg[t][:].indirect(h1_sb[:, lst]), st["pick", u][:, cols], ALU.mult
-                        )
+                    for t, cols, lst, span in gathers(u):
+                        nc.vector.tensor_tensor(picked[:, span], values[t][:].indirect(h1_sb[:, lst]), made["pick", u][:, cols], ALU.mult)
 
-        def each_chunk(k, action):
+        def chunks_at(step, action):
             for j in range(len(chunks)):
-                if chunks[j][4] == k:
+                if chunks[j][3] == step:
                     action(j)
 
+        def by_fours(tile, order):
+            return tile.rearrange(order + " -> p c t i", i=4, t=ROW_TILES)
+
         def add_terms(j):
-            c, r0, width, b0, step = chunks[j]
-            view = lambda x: x[:].rearrange("p (t r) -> p t r", t=4)[:, :, b0 : b0 + OUT_WIDTH].rearrange("p t (c i) -> p c t i", i=4)
-            hid = new("hid", j, pool=wide, dtype=BF16)
-            nc.vector.tensor_tensor(hid[:].rearrange("p (c i t) -> p c t i", i=4, t=4), view(st["hit", c]), view(st["miss", c]), ALU.add)
+            c, r0, b0, step, n = chunks[j]
+            terms = [
+                by_fours(made[name, c][:].rearrange("p (t r) -> p t r", t=ROW_TILES)[:, :, b0 : b0 + n], "p t (c i)")
+                for name in ("picked", "miss")
+            ]
+            hid = new("hid", j, pool=wide, dtype=BF16, width=ROW_TILES * n)
+            nc.vector.tensor_tensor(by_fours(hid[:], "p (c i t)"), terms[0], terms[1], ALU.add)
 
         def last_product(j):
-            codes = new("codes", j, pool=wide, dtype=U32, width=OUT_WIDTH)
-            scales = new("scales", j, pool=wide, dtype=U8, width=OUT_WIDTH)
-            nc.vector.quantize_mx(codes[:].bitcast(FP8X4), scales[:], st["hid", j][:])
-            bank = psum.tile([P, 512], F32, name="bank")
-            for t in range(4):
-                product(bank[:, t * OUT_WIDTH : (t + 1) * OUT_WIDTH], 2, t, codes[:], scales[:])
-            st["bank", j] = bank
+            n = chunks[j][4]
+            codes = new("codes", j, pool=wide, dtype=U32, width=n)
+            scales = new("scales", j, pool=wide, dtype=U8, width=n)
+            nc.vector.quantize_mx(codes[:].bitcast(FP8X4), scales[:], made["hid", j][:])
+            per_bank = PIECE // n
+            made["banks", j] = []
+            for t0 in range(0, ROW_TILES, per_bank):
+                bank = mx_banks.tile([P, PIECE], F32, name="bank")
+                for k in range(per_bank):
+                    product(bank[:, k * n : (k + 1) * n], 2, t0 + k, codes[:], scales[:])
+                made["banks", j].append(bank)
 
-        def leave_bank(j):
-            c, r0, width, b0, step = chunks[j]
-            r = r0 + b0
-            bank = st["bank", j]
-            res = new("res", j, pool=wide, bufs=8)
-            nc.scalar.copy(res[:], bank[:])
-            nc.sync.dma_start(out_rows[:, :, r : r + OUT_WIDTH], res[:].rearrange("p (t r) -> p t r", t=4))
+        def round_result(engine_copy, j):
+            rounded = new("rounded", j, pool=wide, dtype=BF16, width=ROW_TILES * chunks[j][4])
+            engine_copy(by_fours(rounded[:], "p (c i t)"), by_fours(made["res", j][:], "p (t c i)"))
+
+        def leave_banks(j):
+            c, r0, b0, step, n = chunks[j]
+            res = new("res", j, pool=wide, width=ROW_TILES * n)
+            for k, bank in enumerate(made["banks", j]):
+                nc.scalar.copy(res[:, PIECE * k : PIECE * (k + 1)], bank[:])
+            nc.sync.dma_start(out_rows[:, :, r0 + b0 : r0 + b0 + n], res[:].rearrange("p (t r) -> p t r", t=ROW_TILES))
             if j < len(chunks) - LATE_CHUNKS:
-                rounded = new("rounded", j, pool=wide, dtype=BF16)
-                nc.scalar.copy(rounded[:].rearrange("p (c t) -> p c t", t=4), bank[:].rearrange("p (t c) -> p c t", t=4))
+                round_result(nc.scalar.copy, j)
 
         def quantise_result(j):
-            c, r0, width, b0, step = chunks[j]
-            r = r0 + b0
+            c, r0, b0, step, n = chunks[j]
+            cols = slice(r0 + b0, r0 + b0 + n)
             if j >= len(chunks) - LATE_CHUNKS:
-                nc.vector.tensor_copy(
-                    new("rounded", j, pool=wide, dtype=BF16)[:].rearrange("p (c i t) -> p c t i", i=4, t=4),
-                    st["res", j][:].rearrange("p (t c i) -> p c t i", t=4, i=4),
-                )
-            out_codes = new("out_codes", j, pool=wide, dtype=U32, width=OUT_WIDTH, bufs=8)
-            nc.vector.quantize_mx(out_codes[:].bitcast(FP8X4), out_scales[:, r : r + OUT_WIDTH], st["rounded", j][:])
-            nc.sync.dma_start(code_rows[:, r : r + OUT_WIDTH], out_codes[:].bitcast(I32))
+                round_result(nc.vector.tensor_copy, j)
+            out_codes = new("out_codes", j, pool=wide, dtype=U32, width=n, bufs=len(chunks))
+            nc.vector.quantize_mx(out_codes[:].bitcast(FP8X4), out_scales[:, cols], made["rounded", j][:])
+            nc.sync.dma_start(code_rows[:, cols], out_codes[:].bitcast(I32))
 
         fingerprint(0)
-        for k in range(chunks[-1][4] + 2):
+        for k in range(chunks[-1][3] + 2):
             tag_tables(k)
             gap_of(k - 2)
             second_square(k - 1)
             least_of(k - 2)
-            each_chunk(k, add_terms)
+            chunks_at(k, add_terms)
             fetch_second(k)
-            first_difference(k)
-            each_chunk(k, last_product)
+            first_sum(k)
+            chunks_at(k, last_product)
             pick_of(k - 2)
             value_tables(k - 1)
-            second_difference(k)
+            second_sum(k)
             miss_term(k - TERM_LAG)
             first_square(k)
-            each_chunk(k - 1, quantise_result)
-            hit_term(k - TERM_LAG)
+            chunks_at(k - 1, quantise_result)
+            pick_term(k - TERM_LAG)
             fingerprint(k + 1)
             fetch_values(k - 1)
-            each_chunk(k, leave_bank)
+            chunks_at(k, leave_banks)
 
         for q in range(4):
             queue = nc.sync if q % 2 == 0 else nc.scalar

from contextlib import ExitStack

import concourse.mybir as mybir
from concourse.masks import make_identity

F32 = mybir.dt.float32
BF16 = mybir.dt.bfloat16
I32 = mybir.dt.int32
U32 = mybir.dt.uint32
U16 = mybir.dt.uint16
U8 = mybir.dt.uint8
FP8X4 = mybir.dt.float8_e4m3fn_x4
FP4X4 = mybir.dt.float4_e2m1fn_x4
ALU = mybir.AluOpType
ACT = mybir.ActivationFunctionType

P = 128
ROW_TILES = 4
TABLE = 2048
PICKED = 512
QUERIES = 1024
FEATURES = 512
FLOPS = 2 * 512 * FEATURES * (2 * PICKED + QUERIES)

PIECE = 512
CHUNK = 256
GATHER = 256
RANGES = (256, 512, 128, 128)
LATE_PIECES = 2
LATE_CHUNKS = 2
TERM_LAG = 3


def tile_picked_ycuckoo_miss_po_kernel(
    tc, x_words, x_scales, w1_words, w1_scales, w2_words, w2_scales, fp, unit, w3_words, w3_scales, offs, h1, h2,
    out_0, out_1, out_2,
):
    nc = tc.nc
    with ExitStack() as ctx:
        keep = ctx.enter_context(tc.tile_pool(name="keep", bufs=1))
        work = ctx.enter_context(tc.tile_pool(name="work", bufs=4))
        wide = ctx.enter_context(tc.tile_pool(name="wide", bufs=3))
        mx_banks = ctx.enter_context(tc.psum_pool(name="mx_banks", bufs=4))
        turn_banks = ctx.enter_context(tc.psum_pool(name="turn_banks", bufs=2))

        offs_sb = keep.tile([P, PICKED // 16], U16)
        h1_sb = keep.tile([P, QUERIES // 16], U16)
        h2_sb = keep.tile([P, QUERIES // 16], U16)
        xw = keep.tile([P, TABLE], I32)
        xs = keep.tile([P, TABLE], U8)
        xw_picked = keep.tile([P, PICKED], U32, align_bytes=64)
        xs_picked = keep.tile([P, PICKED], U8, align_bytes=64)
        unit_sb = keep.tile([P, ROW_TILES], F32)
        minus_two = keep.tile([P, 1], F32)
        ident = keep.tile([P, P], F32)
        ws_raw = keep.tile([P, 3 * FEATURES], U8)
        ww_raw = [keep.tile([P, 2 * FEATURES], U8, name="ww_raw%d" % i) for i in range(3)]
        ww = [keep.tile([P, 2 * FEATURES], U8, name="ww%d" % i, align_bytes=64) for i in range(3)]
        ws = [keep.tile([P, FEATURES], U8, name="ws%d" % i, align_bytes=64) for i in range(3)]
        tags = [keep.tile([P, PICKED], F32, name="tags%d" % t) for t in range(ROW_TILES)]
        ys = [keep.tile([P, PICKED], F32, name="ys%d" % t) for t in range(ROW_TILES)]
        values = [keep.tile([P, PICKED], F32, name="values%d" % t) for t in range(ROW_TILES)]
        out_scales = keep.tile([P, QUERIES], U8, align_bytes=64)

        w_words = (w1_words, w2_words, w3_words)
        w_scales = (w1_scales, w2_scales, w3_scales)
        fp_rows = fp.rearrange("(p t) r -> p t r", t=ROW_TILES)
        out_rows = out_0.rearrange("(p t) r -> p t r", t=ROW_TILES)
        code_rows = out_1[0].rearrange("p n t -> p (n t)").bitcast(I32)

        pieces = []
        for c, width in enumerate(RANGES):
            nt = PIECE // width
            pieces.extend([(c, sum(RANGES[:c]), width, t0, nt) for t0 in range(0, ROW_TILES, nt)])
        n_pieces = len(pieces)
        chunks = []
        for u, (c, r0, width, t0, nt) in enumerate(pieces):
            if t0 + nt == ROW_TILES:
                apart = 0 if u == n_pieces - 1 else 1
                for b0 in range(0, width, CHUNK):
                    step = u + TERM_LAG + 1 + apart
                    if chunks:
                        step = max(step, chunks[-1][3] + apart)
                    chunks.append((c, r0, b0, step, min(width, CHUNK)))
        fp_sb = [keep.tile([P, PIECE], F32, name="fp%d" % u) for u in range(n_pieces)]

        def load_scales(dst, src):
            for q in range(4):
                nc.sync.dma_start(dst[32 * q : 32 * q + 4, :].bitcast(I32), src[0][4 * q : 4 * q + 4, :].bitcast(I32))

        def load_weight_scales(i):
            load_scales(ws_raw[:, FEATURES * i : FEATURES * (i + 1)], w_scales[i])

        def load_weight_words(i):
            nc.sync.dma_start(ww_raw[i][:].bitcast(I32), w_words[i][0].bitcast(I32))

        def load_fp(u):
            c, r0, width, t0, nt = pieces[u]
            nc.sync.dma_start(fp_sb[u][:].rearrange("p (t r) -> p t r", t=nt), fp_rows[:, t0 : t0 + nt, r0 : r0 + width])

        def deal_words(i):
            nc.vector.tensor_copy(
                ww[i][:].rearrange("p (t m b) -> p t m b", t=ROW_TILES, b=2),
                ww_raw[i][:].rearrange("p (m t b) -> p t m b", t=ROW_TILES, b=2),
            )

        def deal_scales(i):
            nc.vector.tensor_copy(
                ws[i][:].rearrange("p (t m) -> p t m", t=ROW_TILES),
                ws_raw[:, FEATURES * i : FEATURES * (i + 1)].rearrange("p (m t) -> p t m", t=ROW_TILES),
            )

        def product(dst, i, t, codes, scales):
            nc.tensor.matmul_mx(
                dst, lhsT=ww[i][:, 2 * P * t : 2 * P * (t + 1)].bitcast(FP4X4), lhsT_scale=ws[i][:, P * t : P * (t + 1)],
                rhs=codes.bitcast(FP8X4), rhs_scale=scales, start=True, stop=True,
            )

        nc.vector.memset(xs[:].bitcast(I32), 0)
        make_identity(nc, ident[:])
        nc.gpsimd.memset(minus_two[:], -2.0)
        nc.vector.memset(ws_raw[:].bitcast(I32), 0)

        nc.sync.dma_start(offs_sb[:], offs)
        load_weight_words(0)
        load_scales(xs, x_scales)
        nc.sync.dma_start(xw[:], x_words[0].rearrange("p n t -> p (n t)").bitcast(I32))
        load_weight_scales(0)
        load_fp(0)
        nc.sync.dma_start(h1_sb[:], h1)
        nc.sync.dma_start(h2_sb[:], h2)
        load_fp(1)
        load_weight_words(1)
        load_fp(2)
        load_weight_scales(1)
        nc.sync.dma_start(unit_sb[:], unit.rearrange("(p t) o -> p (t o)", t=ROW_TILES))
        load_fp(3)
        load_weight_words(2)
        load_weight_scales(2)
        for u in range(4, n_pieces):
            load_fp(u)

        deal_words(0)
        nc.vector.tensor_copy(xs_picked[:], xs[:].indirect(offs_sb[:]))
        nc.vector.tensor_copy(xw_picked[:], xw[:].bitcast(U32).indirect(offs_sb[:]))
        deal_scales(0)

        made = {}

        def new(name, key, pool=work, dtype=F32, width=PIECE, bufs=None):
            made[name, key] = pool.tile([P, width], dtype, name=name, align_bytes=64, bufs=bufs)
            return made[name, key]

        def live(u):
            return 0 <= u < n_pieces

        def row_tiles_first_met(u):
            return range(pieces[u][3], pieces[u][3] + pieces[u][4]) if live(u) and pieces[u][0] == 0 else ()

        def gathers(u):
            c, r0, width, t0, nt = pieces[u]
            n = min(width, GATHER)
            return [
                (
                    t0 + k // width,
                    slice(k, k + n),
                    slice((r0 + k % width) // 16, (r0 + k % width + n) // 16),
                    slice(t0 * width + k, t0 * width + k + n),
                )
                for k in range(0, PIECE, n)
            ]

        def tag_tables(u):
            for t in row_tiles_first_met(u):
                bank = mx_banks.tile([P, PIECE], F32, name="bank")
                product(bank[:], 0, t, xw_picked[:], xs_picked[:])
                nc.scalar.activation(tags[t][:], bank[:], ACT.Sigmoid, scale=2.0)
                nc.vector.tensor_copy(ys[t][:], bank[:])

        def value_tables(u):
            if u in (0, 1):
                deal_words(u + 1)
                deal_scales(u + 1)
            for t in row_tiles_first_met(u):
                bank = mx_banks.tile([P, PIECE], F32, name="bank")
                product(bank[:], 1, t, xw_picked[:], xs_picked[:])
                nc.scalar.activation(values[t][:], bank[:], ACT.Copy, scale=unit_sb[:, t : t + 1])

        def fingerprint(u):
            if live(u):
                nc.scalar.activation(new("nf", u, bufs=n_pieces)[:], fp_sb[u][:], ACT.Sigmoid, scale=-2.0)

        def fetch_second(u):
            if live(u):
                yb = new("yb", u, bufs=6)
                for t, cols, lst, span in gathers(u):
                    nc.scalar.activation(yb[:, cols], ys[t][:].indirect(h2_sb[:, lst]), ACT.Copy)

        def first_sum(u):
            if live(u):
                d1 = new("d1", u)
                for t, cols, lst, span in gathers(u):
                    nc.vector.tensor_tensor(d1[:, cols], tags[t][:].indirect(h1_sb[:, lst]), made["nf", u][:, cols], ALU.add)

        def second_sum(u):
            if live(u):
                tb = new("tb", u)
                nc.scalar.activation(tb[:], made["yb", u][:], ACT.Sigmoid, scale=2.0)
                d2t = turn_banks.tile([P, PIECE], F32, name="d2t")
                made["d2t", u] = d2t
                for j in range(PIECE // P):
                    cols = slice(P * j, P * (j + 1))
                    nc.tensor.matmul(d2t[:, cols], lhsT=made["nf", u][:, cols], rhs=ident[:], is_transpose=True, start=True, stop=False)
                    nc.tensor.matmul(d2t[:, cols], lhsT=tb[:, cols], rhs=ident[:], is_transpose=True, start=False, stop=True)

        def first_square(u):
            if live(u):
                nc.scalar.activation(new("s1", u)[:], made["d1", u][:], ACT.Square, bias=minus_two[:], scale=2.0)

        def second_square(u):
            if live(u):
                s2t = new("s2t", u)
                nc.scalar.activation(s2t[:], made["d2t", u][:], ACT.Square, bias=minus_two[:], scale=2.0)
                s2 = turn_banks.tile([P, PIECE], F32, name="s2")
                made["s2", u] = s2
                for j in range(PIECE // P):
                    cols = slice(P * j, P * (j + 1))
                    nc.tensor.transpose(s2[:, cols], s2t[:, cols], ident[:])

        def fetch_values(u):
            if n_pieces - LATE_PIECES <= u < n_pieces:
                ga = new("ga", u)
                for t, cols, lst, span in gathers(u):
                    nc.scalar.activation(ga[:, cols], values[t][:].indirect(h1_sb[:, lst]), ACT.Copy)

        def gap_of(u):
            if live(u):
                nc.vector.tensor_tensor(new("gap", u)[:], made["s2", u][:], made["s1", u][:], ALU.subtract)

        def least_of(u):
            if live(u):
                nc.vector.tensor_tensor(new("least", u)[:], made["s2", u][:], made["s1", u][:], ALU.min)

        def pick_of(u):
            if live(u):
                nc.scalar.activation(new("pick", u)[:], made["gap", u][:], ACT.Sigmoid, scale=2.0)

        def miss_term(u):
            if live(u):
                c, r0, width, t0, nt = pieces[u]
                if t0 == 0:
                    new("miss", c, pool=wide, width=ROW_TILES * width)
                for k in range(nt):
                    t = t0 + k
                    cols = slice(k * width, (k + 1) * width)
                    nc.vector.scalar_tensor_tensor(
                        made["miss", c][:, t * width : (t + 1) * width], made["least", u][:, cols], unit_sb[:, t : t + 1],
                        made["yb", u][:, cols], ALU.mult, ALU.mult,
                    )

        def pick_term(u):
            if live(u):
                c, r0, width, t0, nt = pieces[u]
                if t0 == 0:
                    new("picked", c, pool=wide, width=ROW_TILES * width)
                picked = made["picked", c]
                if u >= n_pieces - LATE_PIECES:
                    nc.vector.tensor_tensor(picked[:, t0 * width : (t0 + nt) * width], made["ga", u][:], made["pick", u][:], ALU.mult)
                else:
                    for t, cols, lst, span in gathers(u):
                        nc.vector.tensor_tensor(picked[:, span], values[t][:].indirect(h1_sb[:, lst]), made["pick", u][:, cols], ALU.mult)

        def chunks_at(step, action):
            for j in range(len(chunks)):
                if chunks[j][3] == step:
                    action(j)

        def by_fours(tile, order):
            return tile.rearrange(order + " -> p c t i", i=4, t=ROW_TILES)

        def add_terms(j):
            c, r0, b0, step, n = chunks[j]
            terms = [
                by_fours(made[name, c][:].rearrange("p (t r) -> p t r", t=ROW_TILES)[:, :, b0 : b0 + n], "p t (c i)")
                for name in ("picked", "miss")
            ]
            hid = new("hid", j, pool=wide, dtype=BF16, width=ROW_TILES * n)
            nc.vector.tensor_tensor(by_fours(hid[:], "p (c i t)"), terms[0], terms[1], ALU.add)

        def last_product(j):
            n = chunks[j][4]
            codes = new("codes", j, pool=wide, dtype=U32, width=n)
            scales = new("scales", j, pool=wide, dtype=U8, width=n)
            nc.vector.quantize_mx(codes[:].bitcast(FP8X4), scales[:], made["hid", j][:])
            per_bank = PIECE // n
            made["banks", j] = []
            for t0 in range(0, ROW_TILES, per_bank):
                bank = mx_banks.tile([P, PIECE], F32, name="bank")
                for k in range(per_bank):
                    product(bank[:, k * n : (k + 1) * n], 2, t0 + k, codes[:], scales[:])
                made["banks", j].append(bank)

        def round_result(engine_copy, j):
            rounded = new("rounded", j, pool=wide, dtype=BF16, width=ROW_TILES * chunks[j][4])
            engine_copy(by_fours(rounded[:], "p (c i t)"), by_fours(made["res", j][:], "p (t c i)"))

        def leave_banks(j):
            c, r0, b0, step, n = chunks[j]
            res = new("res", j, pool=wide, width=ROW_TILES * n)
            for k, bank in enumerate(made["banks", j]):
                nc.scalar.copy(res[:, PIECE * k : PIECE * (k + 1)], bank[:])
            nc.sync.dma_start(out_rows[:, :, r0 + b0 : r0 + b0 + n], res[:].rearrange("p (t r) -> p t r", t=ROW_TILES))
            if j < len(chunks) - LATE_CHUNKS:
                round_result(nc.scalar.copy, j)

        def quantise_result(j):
            c, r0, b0, step, n = chunks[j]
            cols = slice(r0 + b0, r0 + b0 + n)
            if j >= len(chunks) - LATE_CHUNKS:
                round_result(nc.vector.tensor_copy, j)
            out_codes = new("out_codes", j, pool=wide, dtype=U32, width=n, bufs=len(chunks))
            nc.vector.quantize_mx(out_codes[:].bitcast(FP8X4), out_scales[:, cols], made["rounded", j][:])
            nc.sync.dma_start(code_rows[:, cols], out_codes[:].bitcast(I32))

        fingerprint(0)
        for k in range(chunks[-1][3] + 2):
            tag_tables(k)
            gap_of(k - 2)
            second_square(k - 1)
            least_of(k - 2)
            chunks_at(k, add_terms)
            fetch_second(k)
            first_sum(k)
            chunks_at(k, last_product)
            pick_of(k - 2)
            value_tables(k - 1)
            second_sum(k)
            miss_term(k - TERM_LAG)
            first_square(k)
            chunks_at(k - 1, quantise_result)
            pick_term(k - TERM_LAG)
            fingerprint(k + 1)
            fetch_values(k - 1)
            chunks_at(k, leave_banks)

        for q in range(4):
            queue = nc.sync if q % 2 == 0 else nc.scalar
            queue.dma_start(out_2[0][4 * q : 4 * q + 4, :].bitcast(I32), out_scales[32 * q : 32 * q + 4, :].bitcast(I32))
